import numpy as np
import ml_dtypes


def mxq(x, axis, fmt="e4m3"):
    dtype, down = {"e4m3": (ml_dtypes.float8_e4m3fn, 7), "e5m2": (ml_dtypes.float8_e5m2, 14)}[fmt]
    v = np.moveaxis(np.asarray(x, np.float32).astype(ml_dtypes.bfloat16).astype(np.float64), axis, -1)
    blocks = v.reshape(v.shape[:-1] + (-1, 32))
    amax = np.abs(blocks).max(-1, keepdims=True)
    byte = np.maximum(np.where(amax > 0, np.frexp(amax)[1] - 1 + 127, 0) - down, 1)
    scale = np.exp2(byte - 127.0)
    codes = (blocks / scale).astype(np.float32).astype(dtype).astype(np.float64)
    return np.moveaxis((codes * scale).reshape(v.shape), -1, axis)


WIDE = False


def mx_kscale(k):
    if not WIDE:
        return np.ones(k)
    levels = np.array([10, -10, 5, -5, 0])
    if k % 512:
        return np.exp2(np.random.permutation(np.resize(levels, k // 32))).repeat(32)
    a = np.empty((k // 512, 16))
    for p in range(k // 512):
        a[p, :8] = np.random.permutation(np.resize(levels, 8))
        for g in range(8):
            far = levels[np.abs(levels - a[p, g]) >= 10]
            a[p, g + 8] = far[np.random.randint(len(far))]
    return np.exp2(a.ravel()).repeat(32)


def f64(x):
    return np.asarray(x).astype(np.float64)


def striped(idx):
    return np.tile(np.asarray(idx).reshape(-1, 16).T, (8, 1)).astype(np.uint16)


def unstriped(offs):
    return offs[:16].T.reshape(-1).astype(np.int64)


E2M1 = np.array([0.0, 0.5, 1.0, 1.5, 2.0, 3.0, 4.0, 6.0, -0.0, -0.5, -1.0, -1.5, -2.0, -3.0, -4.0, -6.0])


def pack_weight(w, fmt):
    k, n = w.shape
    w = f64(np.asarray(w, np.float32).astype(ml_dtypes.bfloat16)).reshape(k // 32, 32, n)
    amax = np.abs(w).max(1)
    if fmt == "e4m3":
        byte = np.frexp(amax)[1] - 1 + 127 - 7
    else:
        mant, ex = np.frexp(amax / 6.0)
        byte = np.where(mant > 0.5, ex, ex - 1) + 127
    byte = np.clip(np.where(amax > 0, byte, 1), 1, 254)
    scaled = (w * np.exp2(127.0 - byte)[:, None, :]).reshape(k, n).astype(np.float32)
    by_word = np.ascontiguousarray(scaled.reshape(k // 512, 128, 4, n).transpose(0, 1, 3, 2))
    if fmt == "e4m3":
        words = by_word.astype(ml_dtypes.float8_e4m3fn).view(np.uint8)
    else:
        c = by_word.astype(ml_dtypes.float4_e2m1fn).view(np.uint8) & 0xF
        words = (c[..., 0::2] | (c[..., 1::2] << 4)).reshape(k // 512, 128, 2 * n)
    return np.ascontiguousarray(words), np.ascontiguousarray(byte.astype(np.uint8).reshape(k // 512, 16, n))


def unpack_weight(words, scales, fmt):
    g, _, n = scales.shape
    words = np.ascontiguousarray(words).reshape(g, 128, n, -1)
    if fmt == "e4m3":
        vals = words.view(ml_dtypes.float8_e4m3fn).astype(np.float64)
    else:
        nib = np.empty((g, 128, n, 4), np.uint8)
        nib[..., 0::2] = words & 0xF
        nib[..., 1::2] = words >> 4
        vals = E2M1[nib]
    vals = vals * np.repeat(np.exp2(scales.astype(np.float64) - 127.0), 8, axis=1)[..., None]
    return vals.transpose(0, 1, 3, 2).reshape(g * 512, n)


D, T, I, J, U, Z, E = 512, 2048, 512, 512, 1024, 1024, 512


def setup_inputs():
    n = np.random.standard_normal
    idx = np.random.permutation(T)[:I]
    idx2 = np.random.permutation(U)[:J]
    idx3 = np.random.permutation(Z)[:J]
    fd = mx_kscale(D)
    fi = mx_kscale(I)
    ti = np.ones(T)
    ti[idx] = fi
    keysp = pack_weight(n((D, T)) / fd[:, None], "e4m3")
    return {
        "keys_words": keysp[0],
        "keys_scales": keysp[1],
        "notes": (n((D, U)) * 1.0 / np.sqrt(D) * fd[:, None]).astype(np.float32),
        "given": (np.random.uniform(0.3, 1.7, (I, Z))).astype(np.float32),
        "rowf": (np.random.uniform(0.02, 0.08, (I, 1)) * fi[:, None]).astype(np.float32),
        "vals": (n((E, T)) / ti).astype(np.float32),
        "mem": (np.random.uniform(0.3, 1.0, (1, J))).astype(np.float32),
        "offs": striped(idx),
        "offs2": striped(idx2),
        "offs3": striped(idx3),
    }


def reference(keys_words, keys_scales, notes, given, rowf, vals, mem, offs, offs2, offs3):
    idx = unstriped(offs)
    idx2 = unstriped(offs2)
    idx3 = unstriped(offs3)
    keysu = unpack_weight(keys_words, keys_scales, "e4m3")
    keysidxg = keysu[:, idx]
    notesidx2q = mxq(f64(notes)[:, idx2], 0, "e4m3")
    g1 = keysidxg.T @ notesidx2q
    g0 = g1 * f64(given)[:, idx3]
    gr1 = g0 * f64(rowf)
    vt1 = f64(vals)[:, idx].T
    vt1q = mxq(vt1, 0, "e4m3")
    gr1q = mxq(gr1, 0, "e4m3")
    o = vt1q.T @ gr1q
    o1 = np.pad(o, ((0, 0), (1, 0)))[:, :J]
    y = o - o1 * f64(mem)
    return y

@@ -1,0 +1,184 @@
+from contextlib import ExitStack
+
+import concourse.mybir as mybir
+from concourse.masks import make_identity
+
+D, T, I, J, U, Z, E = 512, 2048, 512, 512, 1024, 1024, 512
+FLOPS = 2 * D * I * J + 2 * I * E * J
+
+F32 = mybir.dt.float32
+BF16 = mybir.dt.bfloat16
+I32 = mybir.dt.int32
+U32 = mybir.dt.uint32
+U16 = mybir.dt.uint16
+U8 = mybir.dt.uint8
+FP8X4 = mybir.dt.float8_e4m3fn_x4
+MULT = mybir.AluOpType.mult
+SUBTRACT = mybir.AluOpType.subtract
+COPY = mybir.ActivationFunctionType.Copy
+
+P = 128
+PACK = 4
+QUADRANT = 32
+HALF = J // 2
+
+
+def interleave(nc, grouped, planes):
+    nc.vector.tensor_copy(
+        out=grouped[:].rearrange("p (c i) t -> p c t i", i=4),
+        in_=planes[:].rearrange("p t (c i) -> p c t i", i=4),
+    )
+
+
+def quantize(nc, codes, scales, grouped):
+    nc.vector.quantize_mx(
+        out=codes[:].bitcast(FP8X4),
+        scales=scales[:],
+        in_=grouped[:].rearrange("p w t -> p (w t)"),
+    )
+
+
+def tile_attend_tab_timestable_changes_kernel(
+    tc, keys_words, keys_scales, notes, given, rowf, vals, mem, offs, offs2, offs3, out
+):
+    nc = tc.nc
+    with ExitStack() as ctx:
+        keep = ctx.enter_context(tc.tile_pool(name="keep", bufs=1))
+        psum = ctx.enter_context(tc.psum_pool(name="psum", bufs=1))
+
+        token_list = keep.tile([P, I // 16], U16)
+        note_list = keep.tile([P, J // 16], U16)
+        given_list = keep.tile([P, J // 16], U16)
+        key_words = keep.tile([P, T], U32, align_bytes=64)
+        key_scales = keep.tile([P, T], U8, align_bytes=64)
+        note_pool = [keep.tile([P, U], F32, name=f"note_pool{t}") for t in range(PACK)]
+        given_pool = [keep.tile([P, Z], F32, name=f"given_pool{t}") for t in range(PACK)]
+        val_pool = [keep.tile([P, T], F32, name=f"val_pool{b}") for b in range(E // P)]
+        row_factor = keep.tile([P, PACK], F32)
+        mem_rows = keep.tile([P, PACK], F32)
+        identity = keep.tile([P, P], F32)
+
+        notes_by_place = notes.rearrange("(p t) u -> t p u", t=PACK)
+        given_by_place = given.rearrange("(p t) z -> t p z", t=PACK)
+
+        nc.vector.memset(key_scales[:].bitcast(I32), 0)
+        nc.sync.dma_start(note_pool[0][:], notes_by_place[0])
+        nc.sync.dma_start(note_list[:], offs2)
+        nc.sync.dma_start(note_pool[1][:], notes_by_place[1])
+        nc.sync.dma_start(note_pool[2][:], notes_by_place[2])
+        for q in range(P // QUADRANT):
+            nc.sync.dma_start(
+                key_scales[QUADRANT * q : QUADRANT * q + 4, :].bitcast(I32),
+                keys_scales[0, 4 * q : 4 * q + 4, :].bitcast(I32),
+            )
+        nc.sync.dma_start(note_pool[3][:], notes_by_place[3])
+        nc.sync.dma_start(token_list[:], offs)
+        nc.sync.dma_start(
+            key_words[:].bitcast(I32),
+            keys_words[0].rearrange("p c r -> p (c r)").bitcast(I32),
+        )
+        nc.sync.dma_start(row_factor[:], rowf.rearrange("(p t) o -> p (t o)", t=PACK))
+        nc.sync.dma_start(mem_rows[:], mem.rearrange("o (p c) -> (o p) c", c=PACK))
+        nc.sync.dma_start(given_list[:], offs3)
+        for t in range(PACK):
+            nc.sync.dma_start(given_pool[t][:], given_by_place[t])
+        for b in range(E // P):
+            nc.sync.dma_start(val_pool[b][:], vals[b * P : (b + 1) * P, :])
+        make_identity(nc, identity[:])
+
+        note_planes = keep.tile([P, PACK, J], BF16)
+        for t in range(PACK):
+            nc.scalar.activation(note_planes[:, t, :], note_pool[t][:].indirect(note_list[:]), COPY)
+        note_grouped = keep.tile([P, J, PACK], BF16, align_bytes=64)
+        interleave(nc, note_grouped, note_planes)
+
+        key_codes = keep.tile([P, I], U32, align_bytes=64)
+        key_bytes = keep.tile([P, I], U8, align_bytes=64)
+        nc.vector.tensor_copy(
+            key_bytes[:].rearrange("p (t s) -> p s t", t=PACK), key_scales[:].indirect(token_list[:])
+        )
+        note_codes = keep.tile([P, J], U32, align_bytes=64)
+        note_bytes = keep.tile([P, J], U8, align_bytes=64)
+        quantize(nc, note_codes, note_bytes, note_grouped)
+        nc.vector.tensor_copy(
+            key_codes[:].rearrange("p (t s) -> p s t", t=PACK), key_words[:].indirect(token_list[:])
+        )
+
+        mem_turned = psum.tile([P, PACK, P], F32, tag="turned", bufs=2)
+        for c in range(PACK):
+            nc.tensor.transpose(mem_turned[:, c, :], mem_rows[:, c : c + 1].to_broadcast([P, P]), identity[:])
+        mem_wide = keep.tile([P, J], F32)
+        nc.vector.tensor_copy(
+            mem_wide[:].rearrange("p (n c) -> p n c", c=PACK), mem_turned[:].rearrange("p c n -> p n c")
+        )
+        shifted = keep.tile([P, J], F32)
+        nc.vector.memset(shifted[:, 0:1], 0.0)
+
+        table_planes = keep.tile([P, PACK, J], BF16)
+        for t in range(PACK):
+            picked = keep.tile([P, J], F32, name=f"given_picked{t}")
+            nc.scalar.activation(picked[:], given_pool[t][:].indirect(given_list[:]), COPY)
+            scores = psum.tile([P, J], F32, tag="acc", bufs=4)
+            cols = slice(t * P, (t + 1) * P)
+            nc.tensor.matmul_mx(
+                out=scores[:],
+                lhsT=key_codes[:, cols].bitcast(FP8X4),
+                lhsT_scale=key_bytes[:, cols],
+                rhs=note_codes[:].bitcast(FP8X4),
+                rhs_scale=note_bytes[:],
+                start=True,
+                stop=True,
+            )
+            nc.vector.scalar_tensor_tensor(
+                out=table_planes[:, t, :],
+                in0=scores[:],
+                scalar=row_factor[:, t : t + 1],
+                in1=picked[:],
+                op0=MULT,
+                op1=MULT,
+            )
+        table_grouped = keep.tile([P, J, PACK], BF16, align_bytes=64)
+        interleave(nc, table_grouped, table_planes)
+        table_codes = keep.tile([P, J], U32, align_bytes=64)
+        table_bytes = keep.tile([P, J], U8, align_bytes=64)
+        quantize(nc, table_codes, table_bytes, table_grouped)
+
+        for b in range(E // P):
+            val_picked = keep.tile([P, I], BF16, name=f"val_picked{b}")
+            if b < E // P - 1:
+                nc.scalar.activation(val_picked[:], val_pool[b][:].indirect(token_list[:]), COPY)
+            else:
+                nc.scalar.activation(val_picked[:, :256], val_pool[b][:].indirect(token_list[:, :16]), COPY)
+                nc.vector.tensor_copy(val_picked[:, 256:], val_pool[b][:].indirect(token_list[:, 16:]))
+            words = val_picked[:].bitcast(F32)
+            val_turned = psum.tile([P, PACK, P], F32, tag="turned", bufs=2)
+            for u in range(2):
+                nc.tensor.transpose(val_turned[:, u, :], words[:, u : I // 2 : 2], identity[:])
+            val_grouped = keep.tile([P, P, PACK], BF16, align_bytes=64, name=f"val_grouped{b}")
+            nc.scalar.copy(
+                val_grouped[:].rearrange("p e t -> p (e t)").bitcast(F32).rearrange("p (e u) -> p e u", u=2),
+                val_turned[:, 0:2, :].rearrange("p u e -> p e u"),
+            )
+            val_codes = keep.tile([P, P], U32, align_bytes=64, name=f"val_codes{b}")
+            val_bytes = keep.tile([P, P], U8, align_bytes=64, name=f"val_bytes{b}")
+            quantize(nc, val_codes, val_bytes, val_grouped)
+            sums = psum.tile([P, J], F32, tag="acc", bufs=4)
+            nc.tensor.matmul_mx(
+                out=sums[:],
+                lhsT=val_codes[:].bitcast(FP8X4),
+                lhsT_scale=val_bytes[:],
+                rhs=table_codes[:].bitcast(FP8X4),
+                rhs_scale=table_bytes[:],
+                start=True,
+                stop=True,
+            )
+            result = keep.tile([P, J], F32, name=f"result{b}")
+            for lo, hi in ((1, HALF), (HALF, J)):
+                nc.vector.tensor_tensor(shifted[:, lo:hi], sums[:, lo - 1 : hi - 1], mem_wide[:, lo:hi], MULT)
+            for lo in (0, HALF):
+                cols = slice(lo, lo + HALF)
+                nc.vector.tensor_tensor(result[:, cols], sums[:, cols], shifted[:, cols], SUBTRACT)
+                if b == E // P - 1:
+                    nc.sync.dma_start(out[b * P : (b + 1) * P, cols], result[:, cols])
+            if b < E // P - 1:
+                nc.sync.dma_start(out[b * P : (b + 1) * P, :], result[:])

@@ -65,20 +65,20 @@ def tile_attend_tab_timestable_changes_kernel(
         nc.sync.dma_start(note_pool[0][:], notes_by_place[0])
         nc.sync.dma_start(note_list[:], offs2)
         nc.sync.dma_start(note_pool[1][:], notes_by_place[1])
+        nc.sync.dma_start(token_list[:], offs)
         nc.sync.dma_start(note_pool[2][:], notes_by_place[2])
+        nc.sync.dma_start(note_pool[3][:], notes_by_place[3])
+        nc.scalar.dma_start(mem_rows[:], mem.rearrange("o (p c) -> (o p) c", c=PACK))
+        nc.scalar.dma_start(row_factor[:], rowf.rearrange("(p t) o -> p (t o)", t=PACK))
         for q in range(P // QUADRANT):
-            nc.sync.dma_start(
+            nc.scalar.dma_start(
                 key_scales[QUADRANT * q : QUADRANT * q + 4, :].bitcast(I32),
                 keys_scales[0, 4 * q : 4 * q + 4, :].bitcast(I32),
             )
-        nc.sync.dma_start(note_pool[3][:], notes_by_place[3])
-        nc.sync.dma_start(token_list[:], offs)
         nc.sync.dma_start(
             key_words[:].bitcast(I32),
             keys_words[0].rearrange("p c r -> p (c r)").bitcast(I32),
         )
-        nc.sync.dma_start(row_factor[:], rowf.rearrange("(p t) o -> p (t o)", t=PACK))
-        nc.sync.dma_start(mem_rows[:], mem.rearrange("o (p c) -> (o p) c", c=PACK))
         nc.sync.dma_start(given_list[:], offs3)
         for t in range(PACK):
             nc.sync.dma_start(given_pool[t][:], given_by_place[t])
@@ -88,7 +88,11 @@ def tile_attend_tab_timestable_changes_kernel(
 
         note_planes = keep.tile([P, PACK, J], BF16)
         for t in range(PACK):
-            nc.scalar.activation(note_planes[:, t, :], note_pool[t][:].indirect(note_list[:]), COPY)
+            listed = note_pool[t][:].indirect(note_list[:])
+            if t in (0, PACK - 1):
+                nc.scalar.activation(note_planes[:, t, :], listed, COPY)
+            else:
+                nc.vector.tensor_copy(note_planes[:, t, :], listed)
         note_grouped = keep.tile([P, J, PACK], BF16, align_bytes=64)
         interleave(nc, note_grouped, note_planes)
 
@@ -118,7 +122,7 @@ def tile_attend_tab_timestable_changes_kernel(
         for t in range(PACK):
             picked = keep.tile([P, J], F32, name=f"given_picked{t}")
             nc.scalar.activation(picked[:], given_pool[t][:].indirect(given_list[:]), COPY)
-            scores = psum.tile([P, J], F32, tag="acc", bufs=4)
+            scores = psum.tile([P, J], F32, tag="acc", bufs=6)
             cols = slice(t * P, (t + 1) * P)
             nc.tensor.matmul_mx(
                 out=scores[:],
@@ -143,42 +147,53 @@ def tile_attend_tab_timestable_changes_kernel(
         table_bytes = keep.tile([P, J], U8, align_bytes=64)
         quantize(nc, table_codes, table_bytes, table_grouped)
 
-        for b in range(E // P):
+        blocks = E // P
+        results = [keep.tile([P, J], F32, align_bytes=64, name=f"result{b}") for b in range(blocks)]
+        first_grouped = keep.tile([P, HALF], F32, align_bytes=64)
+
+        def finish(b, lo, sums):
+            cols = slice(lo, lo + sums.shape[1])
+            nc.vector.tensor_tensor(results[b][:, cols], sums[:], shifted[:, cols], SUBTRACT)
+            nc.sync.dma_start(out[b * P : (b + 1) * P, cols], results[b][:, cols])
+
+        pieces = []
+        for b in range(blocks):
+            last = b == blocks - 1
             val_picked = keep.tile([P, I], BF16, name=f"val_picked{b}")
-            if b < E // P - 1:
-                nc.scalar.activation(val_picked[:], val_pool[b][:].indirect(token_list[:]), COPY)
-            else:
-                nc.scalar.activation(val_picked[:, :256], val_pool[b][:].indirect(token_list[:, :16]), COPY)
-                nc.vector.tensor_copy(val_picked[:, 256:], val_pool[b][:].indirect(token_list[:, 16:]))
+            nc.scalar.activation(val_picked[:], val_pool[b][:].indirect(token_list[:]), COPY)
             words = val_picked[:].bitcast(F32)
             val_turned = psum.tile([P, PACK, P], F32, tag="turned", bufs=2)
             for u in range(2):
                 nc.tensor.transpose(val_turned[:, u, :], words[:, u : I // 2 : 2], identity[:])
-            val_grouped = keep.tile([P, P, PACK], BF16, align_bytes=64, name=f"val_grouped{b}")
-            nc.scalar.copy(
-                val_grouped[:].rearrange("p e t -> p (e t)").bitcast(F32).rearrange("p (e u) -> p e u", u=2),
+            val_grouped = results[b - 1][:, HALF:] if b > 0 else first_grouped[:]
+            copy_words = nc.scalar.copy if last else nc.vector.tensor_copy
+            copy_words(
+                val_grouped.rearrange("p (e u) -> p e u", u=2),
                 val_turned[:, 0:2, :].rearrange("p u e -> p e u"),
             )
             val_codes = keep.tile([P, P], U32, align_bytes=64, name=f"val_codes{b}")
             val_bytes = keep.tile([P, P], U8, align_bytes=64, name=f"val_bytes{b}")
-            quantize(nc, val_codes, val_bytes, val_grouped)
-            sums = psum.tile([P, J], F32, tag="acc", bufs=4)
-            nc.tensor.matmul_mx(
-                out=sums[:],
-                lhsT=val_codes[:].bitcast(FP8X4),
-                lhsT_scale=val_bytes[:],
-                rhs=table_codes[:].bitcast(FP8X4),
-                rhs_scale=table_bytes[:],
-                start=True,
-                stop=True,
-            )
-            result = keep.tile([P, J], F32, name=f"result{b}")
-            for lo, hi in ((1, HALF), (HALF, J)):
-                nc.vector.tensor_tensor(shifted[:, lo:hi], sums[:, lo - 1 : hi - 1], mem_wide[:, lo:hi], MULT)
-            for lo in (0, HALF):
-                cols = slice(lo, lo + HALF)
-                nc.vector.tensor_tensor(result[:, cols], sums[:, cols], shifted[:, cols], SUBTRACT)
-                if b == E // P - 1:
-                    nc.sync.dma_start(out[b * P : (b + 1) * P, cols], result[:, cols])
-            if b < E // P - 1:
-                nc.sync.dma_start(out[b * P : (b + 1) * P, :], result[:])
+            nc.vector.quantize_mx(out=val_codes[:].bitcast(FP8X4), scales=val_bytes[:], in_=val_grouped.bitcast(BF16))
+            for lo, sums in pieces:
+                finish(b - 1, lo, sums)
+            width = HALF if last else J
+            pieces = []
+            for lo in range(0, J, width):
+                sums = psum.tile([P, width], F32, tag="acc", bufs=6)
+                nc.tensor.matmul_mx(
+                    out=sums[:],
+                    lhsT=val_codes[:].bitcast(FP8X4),
+                    lhsT_scale=val_bytes[:],
+                    rhs=table_codes[:, lo : lo + width].bitcast(FP8X4),
+                    rhs_scale=table_bytes[:, lo : lo + width],
+                    start=True,
+                    stop=True,
+                )
+                pieces.append((lo, sums))
+            for lo, sums in pieces:
+                n = min(width, J - 1 - lo)
+                nc.vector.tensor_tensor(
+                    shifted[:, lo + 1 : lo + 1 + n], sums[:, :n], mem_wide[:, lo + 1 : lo + 1 + n], MULT
+                )
+        for lo, sums in pieces:
+            finish(blocks - 1, lo, sums)

@@ -21,6 +21,8 @@ P = 128
 PACK = 4
 QUADRANT = 32
 HALF = J // 2
+NOTE_SHARE = (J, J, J, HALF)
+GIVEN_SHARE = (J, J, J, HALF)
 
 
 def interleave(nc, grouped, planes):
@@ -28,6 +30,14 @@ def interleave(nc, grouped, planes):
         out=grouped[:].rearrange("p (c i) t -> p c t i", i=4),
         in_=planes[:].rearrange("p t (c i) -> p c t i", i=4),
     )
+
+
+def gather(nc, picked, window, offsets, on_scalar):
+    n = picked.shape[1]
+    if on_scalar > 0:
+        nc.scalar.activation(picked[:, :on_scalar], window[:].indirect(offsets[:, : on_scalar // 16]), COPY)
+    if on_scalar < n:
+        nc.vector.tensor_copy(picked[:, on_scalar:], window[:].indirect(offsets[:, on_scalar // 16 :]))
 
 
 def quantize(nc, codes, scales, grouped):
@@ -61,38 +71,43 @@ def tile_attend_tab_timestable_changes_kernel(
         notes_by_place = notes.rearrange("(p t) u -> t p u", t=PACK)
         given_by_place = given.rearrange("(p t) z -> t p z", t=PACK)
 
-        nc.vector.memset(key_scales[:].bitcast(I32), 0)
+        shifted = [keep.tile([P, J], F32, name=f"shifted{k}") for k in range(2)]
+        nc.vector.memset(shifted[0][:, 0:1], 0.0)
+        nc.scalar.activation(shifted[1][:, 0:1], shifted[0][:, 0:1], COPY)
+        scale_rows = keep.tile([P, 2, T // 4], I32)
         nc.sync.dma_start(note_pool[0][:], notes_by_place[0])
         nc.sync.dma_start(note_list[:], offs2)
+        for h in range(2):
+            nc.sync.dma_start(
+                scale_rows[64 * h : 64 * h + 4],
+                keys_scales[0, 8 * h : 8 * h + 8, :].bitcast(I32).rearrange("(q r) c -> r q c", r=4),
+            )
         nc.sync.dma_start(note_pool[1][:], notes_by_place[1])
         nc.sync.dma_start(token_list[:], offs)
         nc.sync.dma_start(note_pool[2][:], notes_by_place[2])
         nc.sync.dma_start(note_pool[3][:], notes_by_place[3])
-        nc.scalar.dma_start(mem_rows[:], mem.rearrange("o (p c) -> (o p) c", c=PACK))
-        nc.scalar.dma_start(row_factor[:], rowf.rearrange("(p t) o -> p (t o)", t=PACK))
-        for q in range(P // QUADRANT):
-            nc.scalar.dma_start(
-                key_scales[QUADRANT * q : QUADRANT * q + 4, :].bitcast(I32),
-                keys_scales[0, 4 * q : 4 * q + 4, :].bitcast(I32),
-            )
+        nc.sync.dma_start(mem_rows[:], mem.rearrange("o (p c) -> (o p) c", c=PACK))
         nc.sync.dma_start(
             key_words[:].bitcast(I32),
             keys_words[0].rearrange("p c r -> p (c r)").bitcast(I32),
         )
         nc.sync.dma_start(given_list[:], offs3)
+        nc.sync.dma_start(row_factor[:], rowf.rearrange("(p t) o -> p (t o)", t=PACK))
         for t in range(PACK):
             nc.sync.dma_start(given_pool[t][:], given_by_place[t])
         for b in range(E // P):
             nc.sync.dma_start(val_pool[b][:], vals[b * P : (b + 1) * P, :])
+        nc.vector.memset(key_scales[:].bitcast(I32), 0)
+        for q in range(P // QUADRANT):
+            src = 64 * (q // 2)
+            nc.vector.tensor_copy(
+                key_scales[QUADRANT * q : QUADRANT * q + 4, :].bitcast(I32), scale_rows[src : src + 4, q % 2, :]
+            )
         make_identity(nc, identity[:])
 
         note_planes = keep.tile([P, PACK, J], BF16)
         for t in range(PACK):
-            listed = note_pool[t][:].indirect(note_list[:])
-            if t in (0, PACK - 1):
-                nc.scalar.activation(note_planes[:, t, :], listed, COPY)
-            else:
-                nc.vector.tensor_copy(note_planes[:, t, :], listed)
+            gather(nc, note_planes[:, t, :], note_pool[t], note_list, NOTE_SHARE[t])
         note_grouped = keep.tile([P, J, PACK], BF16, align_bytes=64)
         interleave(nc, note_grouped, note_planes)
 
@@ -115,13 +130,11 @@ def tile_attend_tab_timestable_changes_kernel(
         nc.vector.tensor_copy(
             mem_wide[:].rearrange("p (n c) -> p n c", c=PACK), mem_turned[:].rearrange("p c n -> p n c")
         )
-        shifted = keep.tile([P, J], F32)
-        nc.vector.memset(shifted[:, 0:1], 0.0)
 
         table_planes = keep.tile([P, PACK, J], BF16)
         for t in range(PACK):
             picked = keep.tile([P, J], F32, name=f"given_picked{t}")
-            nc.scalar.activation(picked[:], given_pool[t][:].indirect(given_list[:]), COPY)
+            gather(nc, picked[:], given_pool[t], given_list, GIVEN_SHARE[t])
             scores = psum.tile([P, J], F32, tag="acc", bufs=6)
             cols = slice(t * P, (t + 1) * P)
             nc.tensor.matmul_mx(
@@ -148,36 +161,32 @@ def tile_attend_tab_timestable_changes_kernel(
         quantize(nc, table_codes, table_bytes, table_grouped)
 
         blocks = E // P
+        last = blocks - 1
         results = [keep.tile([P, J], F32, align_bytes=64, name=f"result{b}") for b in range(blocks)]
-        first_grouped = keep.tile([P, HALF], F32, align_bytes=64)
+        turned, grouped, pieces = {}, {}, {}
 
-        def finish(b, lo, sums):
-            cols = slice(lo, lo + sums.shape[1])
-            nc.vector.tensor_tensor(results[b][:, cols], sums[:], shifted[:, cols], SUBTRACT)
-            nc.sync.dma_start(out[b * P : (b + 1) * P, cols], results[b][:, cols])
-
-        pieces = []
-        for b in range(blocks):
-            last = b == blocks - 1
-            val_picked = keep.tile([P, I], BF16, name=f"val_picked{b}")
+        def turn(b):
+            val_picked = keep.tile([P, I], BF16, tag=f"picked{b}", align_bytes=64)
             nc.scalar.activation(val_picked[:], val_pool[b][:].indirect(token_list[:]), COPY)
             words = val_picked[:].bitcast(F32)
-            val_turned = psum.tile([P, PACK, P], F32, tag="turned", bufs=2)
+            turned[b] = psum.tile([P, 2, P], F32, tag="turned", bufs=2, name="val_turned")
             for u in range(2):
-                nc.tensor.transpose(val_turned[:, u, :], words[:, u : I // 2 : 2], identity[:])
-            val_grouped = results[b - 1][:, HALF:] if b > 0 else first_grouped[:]
-            copy_words = nc.scalar.copy if last else nc.vector.tensor_copy
-            copy_words(
-                val_grouped.rearrange("p (e u) -> p e u", u=2),
-                val_turned[:, 0:2, :].rearrange("p u e -> p e u"),
-            )
-            val_codes = keep.tile([P, P], U32, align_bytes=64, name=f"val_codes{b}")
+                nc.tensor.transpose(turned[b][:, u, :], words[:, u : I // 2 : 2], identity[:])
+
+        def group(b, share):
+            if share:
+                grouped[b] = results[b - 1][:, HALF:]
+            else:
+                grouped[b] = keep.tile([P, HALF], F32, align_bytes=64, name=f"val_grouped{b}")[:]
+            copy_words = nc.scalar.copy if b == last else nc.vector.tensor_copy
+            copy_words(grouped[b].rearrange("p (e u) -> p e u", u=2), turned[b][:].rearrange("p u e -> p e u"))
+
+        def multiply(b, held):
+            val_codes = keep.tile([P, P], U32, align_bytes=64, tag=f"picked{b + 1}" if held else f"codes{b}")
             val_bytes = keep.tile([P, P], U8, align_bytes=64, name=f"val_bytes{b}")
-            nc.vector.quantize_mx(out=val_codes[:].bitcast(FP8X4), scales=val_bytes[:], in_=val_grouped.bitcast(BF16))
-            for lo, sums in pieces:
-                finish(b - 1, lo, sums)
-            width = HALF if last else J
-            pieces = []
+            nc.vector.quantize_mx(out=val_codes[:].bitcast(FP8X4), scales=val_bytes[:], in_=grouped[b].bitcast(BF16))
+            width = HALF if b == last else J
+            pieces[b] = []
             for lo in range(0, J, width):
                 sums = psum.tile([P, width], F32, tag="acc", bufs=6)
                 nc.tensor.matmul_mx(
@@ -189,11 +198,38 @@ def tile_attend_tab_timestable_changes_kernel(
                     start=True,
                     stop=True,
                 )
-                pieces.append((lo, sums))
-            for lo, sums in pieces:
-                n = min(width, J - 1 - lo)
+                pieces[b].append((lo, sums))
+
+        def shift(b):
+            for lo, sums in pieces[b]:
+                n = min(sums.shape[1], J - 1 - lo)
                 nc.vector.tensor_tensor(
-                    shifted[:, lo + 1 : lo + 1 + n], sums[:, :n], mem_wide[:, lo + 1 : lo + 1 + n], MULT
+                    shifted[b % 2][:, lo + 1 : lo + 1 + n], sums[:, :n], mem_wide[:, lo + 1 : lo + 1 + n], MULT
                 )
-        for lo, sums in pieces:
-            finish(blocks - 1, lo, sums)
+
+        def finish(b):
+            for lo, sums in pieces[b]:
+                cols = slice(lo, lo + sums.shape[1])
+                nc.vector.tensor_tensor(results[b][:, cols], sums[:], shifted[b % 2][:, cols], SUBTRACT)
+                nc.sync.dma_start(out[b * P : (b + 1) * P, cols], results[b][:, cols])
+
+        turn(0)
+        group(0, False)
+        multiply(0, False)
+        turn(1)
+        shift(0)
+        finish(0)
+        group(1, False)
+        turn(2)
+        multiply(1, True)
+        group(2, False)
+        multiply(2, False)
+        turn(3)
+        shift(1)
+        shift(2)
+        finish(1)
+        group(3, True)
+        multiply(3, False)
+        finish(2)
+        shift(3)
+        finish(3)

@@ -22,13 +22,13 @@ PACK = 4
 QUADRANT = 32
 HALF = J // 2
 NOTE_SHARE = (J, J, J, HALF)
-GIVEN_SHARE = (J, J, J, HALF)
+GIVEN_SHARE = (J, J, J, J)
 
 
-def interleave(nc, grouped, planes):
+def interleave(nc, grouped, planes, cols):
     nc.vector.tensor_copy(
-        out=grouped[:].rearrange("p (c i) t -> p c t i", i=4),
-        in_=planes[:].rearrange("p t (c i) -> p c t i", i=4),
+        out=grouped[:, cols, :].rearrange("p (c i) t -> p c t i", i=4),
+        in_=planes[:, :, cols].rearrange("p t (c i) -> p c t i", i=4),
     )
 
 
@@ -77,6 +77,7 @@ def tile_attend_tab_timestable_changes_kernel(
         scale_rows = keep.tile([P, 2, T // 4], I32)
         nc.sync.dma_start(note_pool[0][:], notes_by_place[0])
         nc.sync.dma_start(note_list[:], offs2)
+        nc.sync.dma_start(mem_rows[:], mem.rearrange("o (p c) -> (o p) c", c=PACK))
         for h in range(2):
             nc.sync.dma_start(
                 scale_rows[64 * h : 64 * h + 4],
@@ -86,7 +87,6 @@ def tile_attend_tab_timestable_changes_kernel(
         nc.sync.dma_start(token_list[:], offs)
         nc.sync.dma_start(note_pool[2][:], notes_by_place[2])
         nc.sync.dma_start(note_pool[3][:], notes_by_place[3])
-        nc.sync.dma_start(mem_rows[:], mem.rearrange("o (p c) -> (o p) c", c=PACK))
         nc.sync.dma_start(
             key_words[:].bitcast(I32),
             keys_words[0].rearrange("p c r -> p (c r)").bitcast(I32),
@@ -105,11 +105,19 @@ def tile_attend_tab_timestable_changes_kernel(
             )
         make_identity(nc, identity[:])
 
+        mem_turned = psum.tile([P, PACK, P], F32, tag="turned", bufs=2)
+        for c in range(PACK):
+            nc.tensor.transpose(mem_turned[:, c, :], mem_rows[:, c : c + 1].to_broadcast([P, P]), identity[:])
+        mem_wide = keep.tile([P, J], F32)
+        nc.vector.tensor_copy(
+            mem_wide[:].rearrange("p (n c) -> p n c", c=PACK), mem_turned[:].rearrange("p c n -> p n c")
+        )
+
         note_planes = keep.tile([P, PACK, J], BF16)
         for t in range(PACK):
             gather(nc, note_planes[:, t, :], note_pool[t], note_list, NOTE_SHARE[t])
         note_grouped = keep.tile([P, J, PACK], BF16, align_bytes=64)
-        interleave(nc, note_grouped, note_planes)
+        interleave(nc, note_grouped, note_planes, slice(0, J))
 
         key_codes = keep.tile([P, I], U32, align_bytes=64)
         key_bytes = keep.tile([P, I], U8, align_bytes=64)
@@ -121,14 +129,6 @@ def tile_attend_tab_timestable_changes_kernel(
         quantize(nc, note_codes, note_bytes, note_grouped)
         nc.vector.tensor_copy(
             key_codes[:].rearrange("p (t s) -> p s t", t=PACK), key_words[:].indirect(token_list[:])
-        )
-
-        mem_turned = psum.tile([P, PACK, P], F32, tag="turned", bufs=2)
-        for c in range(PACK):
-            nc.tensor.transpose(mem_turned[:, c, :], mem_rows[:, c : c + 1].to_broadcast([P, P]), identity[:])
-        mem_wide = keep.tile([P, J], F32)
-        nc.vector.tensor_copy(
-            mem_wide[:].rearrange("p (n c) -> p n c", c=PACK), mem_turned[:].rearrange("p c n -> p n c")
         )
 
         table_planes = keep.tile([P, PACK, J], BF16)
@@ -155,10 +155,17 @@ def tile_attend_tab_timestable_changes_kernel(
                 op1=MULT,
             )
         table_grouped = keep.tile([P, J, PACK], BF16, align_bytes=64)
-        interleave(nc, table_grouped, table_planes)
+        halves = (slice(0, HALF), slice(HALF, J))
+        for cols in halves:
+            interleave(nc, table_grouped, table_planes, cols)
         table_codes = keep.tile([P, J], U32, align_bytes=64)
         table_bytes = keep.tile([P, J], U8, align_bytes=64)
-        quantize(nc, table_codes, table_bytes, table_grouped)
+        for cols in halves:
+            nc.vector.quantize_mx(
+                out=table_codes[:, cols].bitcast(FP8X4),
+                scales=table_bytes[:, cols],
+                in_=table_grouped[:, cols, :].rearrange("p w t -> p (w t)"),
+            )
 
         blocks = E // P
         last = blocks - 1
@@ -178,7 +185,7 @@ def tile_attend_tab_timestable_changes_kernel(
                 grouped[b] = results[b - 1][:, HALF:]
             else:
                 grouped[b] = keep.tile([P, HALF], F32, align_bytes=64, name=f"val_grouped{b}")[:]
-            copy_words = nc.scalar.copy if b == last else nc.vector.tensor_copy
+            copy_words = nc.scalar.copy if b in (0, last) else nc.vector.tensor_copy
             copy_words(grouped[b].rearrange("p (e u) -> p e u", u=2), turned[b][:].rearrange("p u e -> p e u"))
 
         def multiply(b, held):

from contextlib import ExitStack

import concourse.mybir as mybir
from concourse.masks import make_identity

D, T, I, J, U, Z, E = 512, 2048, 512, 512, 1024, 1024, 512
FLOPS = 2 * D * I * J + 2 * I * E * J

F32 = mybir.dt.float32
BF16 = mybir.dt.bfloat16
I32 = mybir.dt.int32
U32 = mybir.dt.uint32
U16 = mybir.dt.uint16
U8 = mybir.dt.uint8
FP8X4 = mybir.dt.float8_e4m3fn_x4
MULT = mybir.AluOpType.mult
SUBTRACT = mybir.AluOpType.subtract
COPY = mybir.ActivationFunctionType.Copy

P = 128
PACK = 4
QUADRANT = 32
HALF = J // 2
NOTE_SHARE = (J, J, J, HALF)
GIVEN_SHARE = (J, J, J, J)


def interleave(nc, grouped, planes, cols):
    nc.vector.tensor_copy(
        out=grouped[:, cols, :].rearrange("p (c i) t -> p c t i", i=4),
        in_=planes[:, :, cols].rearrange("p t (c i) -> p c t i", i=4),
    )


def gather(nc, picked, window, offsets, on_scalar):
    n = picked.shape[1]
    if on_scalar > 0:
        nc.scalar.activation(picked[:, :on_scalar], window[:].indirect(offsets[:, : on_scalar // 16]), COPY)
    if on_scalar < n:
        nc.vector.tensor_copy(picked[:, on_scalar:], window[:].indirect(offsets[:, on_scalar // 16 :]))


def quantize(nc, codes, scales, grouped):
    nc.vector.quantize_mx(
        out=codes[:].bitcast(FP8X4),
        scales=scales[:],
        in_=grouped[:].rearrange("p w t -> p (w t)"),
    )


def tile_attend_tab_timestable_changes_kernel(
    tc, keys_words, keys_scales, notes, given, rowf, vals, mem, offs, offs2, offs3, out
):
    nc = tc.nc
    with ExitStack() as ctx:
        keep = ctx.enter_context(tc.tile_pool(name="keep", bufs=1))
        psum = ctx.enter_context(tc.psum_pool(name="psum", bufs=1))

        token_list = keep.tile([P, I // 16], U16)
        note_list = keep.tile([P, J // 16], U16)
        given_list = keep.tile([P, J // 16], U16)
        key_words = keep.tile([P, T], U32, align_bytes=64)
        key_scales = keep.tile([P, T], U8, align_bytes=64)
        note_pool = [keep.tile([P, U], F32, name=f"note_pool{t}") for t in range(PACK)]
        given_pool = [keep.tile([P, Z], F32, name=f"given_pool{t}") for t in range(PACK)]
        val_pool = [keep.tile([P, T], F32, name=f"val_pool{b}") for b in range(E // P)]
        row_factor = keep.tile([P, PACK], F32)
        mem_rows = keep.tile([P, PACK], F32)
        identity = keep.tile([P, P], F32)

        notes_by_place = notes.rearrange("(p t) u -> t p u", t=PACK)
        given_by_place = given.rearrange("(p t) z -> t p z", t=PACK)

        shifted = [keep.tile([P, J], F32, name=f"shifted{k}") for k in range(2)]
        nc.vector.memset(shifted[0][:, 0:1], 0.0)
        nc.scalar.activation(shifted[1][:, 0:1], shifted[0][:, 0:1], COPY)
        scale_rows = keep.tile([P, 2, T // 4], I32)
        nc.sync.dma_start(note_pool[0][:], notes_by_place[0])
        nc.sync.dma_start(note_list[:], offs2)
        nc.sync.dma_start(mem_rows[:], mem.rearrange("o (p c) -> (o p) c", c=PACK))
        for h in range(2):
            nc.sync.dma_start(
                scale_rows[64 * h : 64 * h + 4],
                keys_scales[0, 8 * h : 8 * h + 8, :].bitcast(I32).rearrange("(q r) c -> r q c", r=4),
            )
        nc.sync.dma_start(note_pool[1][:], notes_by_place[1])
        nc.sync.dma_start(token_list[:], offs)
        nc.sync.dma_start(note_pool[2][:], notes_by_place[2])
        nc.sync.dma_start(note_pool[3][:], notes_by_place[3])
        nc.sync.dma_start(
            key_words[:].bitcast(I32),
            keys_words[0].rearrange("p c r -> p (c r)").bitcast(I32),
        )
        nc.sync.dma_start(given_list[:], offs3)
        nc.sync.dma_start(row_factor[:], rowf.rearrange("(p t) o -> p (t o)", t=PACK))
        for t in range(PACK):
            nc.sync.dma_start(given_pool[t][:], given_by_place[t])
        for b in range(E // P):
            nc.sync.dma_start(val_pool[b][:], vals[b * P : (b + 1) * P, :])
        nc.vector.memset(key_scales[:].bitcast(I32), 0)
        for q in range(P // QUADRANT):
            src = 64 * (q // 2)
            nc.vector.tensor_copy(
                key_scales[QUADRANT * q : QUADRANT * q + 4, :].bitcast(I32), scale_rows[src : src + 4, q % 2, :]
            )
        make_identity(nc, identity[:])

        mem_turned = psum.tile([P, PACK, P], F32, tag="turned", bufs=2)
        for c in range(PACK):
            nc.tensor.transpose(mem_turned[:, c, :], mem_rows[:, c : c + 1].to_broadcast([P, P]), identity[:])
        mem_wide = keep.tile([P, J], F32)
        nc.vector.tensor_copy(
            mem_wide[:].rearrange("p (n c) -> p n c", c=PACK), mem_turned[:].rearrange("p c n -> p n c")
        )

        note_planes = keep.tile([P, PACK, J], BF16)
        for t in range(PACK):
            gather(nc, note_planes[:, t, :], note_pool[t], note_list, NOTE_SHARE[t])
        note_grouped = keep.tile([P, J, PACK], BF16, align_bytes=64)
        interleave(nc, note_grouped, note_planes, slice(0, J))

        key_codes = keep.tile([P, I], U32, align_bytes=64)
        key_bytes = keep.tile([P, I], U8, align_bytes=64)
        nc.vector.tensor_copy(
            key_bytes[:].rearrange("p (t s) -> p s t", t=PACK), key_scales[:].indirect(token_list[:])
        )
        note_codes = keep.tile([P, J], U32, align_bytes=64)
        note_bytes = keep.tile([P, J], U8, align_bytes=64)
        quantize(nc, note_codes, note_bytes, note_grouped)
        nc.vector.tensor_copy(
            key_codes[:].rearrange("p (t s) -> p s t", t=PACK), key_words[:].indirect(token_list[:])
        )

        table_planes = keep.tile([P, PACK, J], BF16)
        for t in range(PACK):
            picked = keep.tile([P, J], F32, name=f"given_picked{t}")
            gather(nc, picked[:], given_pool[t], given_list, GIVEN_SHARE[t])
            scores = psum.tile([P, J], F32, tag="acc", bufs=6)
            cols = slice(t * P, (t + 1) * P)
            nc.tensor.matmul_mx(
                out=scores[:],
                lhsT=key_codes[:, cols].bitcast(FP8X4),
                lhsT_scale=key_bytes[:, cols],
                rhs=note_codes[:].bitcast(FP8X4),
                rhs_scale=note_bytes[:],
                start=True,
                stop=True,
            )
            nc.vector.scalar_tensor_tensor(
                out=table_planes[:, t, :],
                in0=scores[:],
                scalar=row_factor[:, t : t + 1],
                in1=picked[:],
                op0=MULT,
                op1=MULT,
            )
        table_grouped = keep.tile([P, J, PACK], BF16, align_bytes=64)
        halves = (slice(0, HALF), slice(HALF, J))
        for cols in halves:
            interleave(nc, table_grouped, table_planes, cols)
        table_codes = keep.tile([P, J], U32, align_bytes=64)
        table_bytes = keep.tile([P, J], U8, align_bytes=64)
        for cols in halves:
            nc.vector.quantize_mx(
                out=table_codes[:, cols].bitcast(FP8X4),
                scales=table_bytes[:, cols],
                in_=table_grouped[:, cols, :].rearrange("p w t -> p (w t)"),
            )

        blocks = E // P
        last = blocks - 1
        results = [keep.tile([P, J], F32, align_bytes=64, name=f"result{b}") for b in range(blocks)]
        turned, grouped, pieces = {}, {}, {}

        def turn(b):
            val_picked = keep.tile([P, I], BF16, tag=f"picked{b}", align_bytes=64)
            nc.scalar.activation(val_picked[:], val_pool[b][:].indirect(token_list[:]), COPY)
            words = val_picked[:].bitcast(F32)
            turned[b] = psum.tile([P, 2, P], F32, tag="turned", bufs=2, name="val_turned")
            for u in range(2):
                nc.tensor.transpose(turned[b][:, u, :], words[:, u : I // 2 : 2], identity[:])

        def group(b, share):
            if share:
                grouped[b] = results[b - 1][:, HALF:]
            else:
                grouped[b] = keep.tile([P, HALF], F32, align_bytes=64, name=f"val_grouped{b}")[:]
            copy_words = nc.scalar.copy if b in (0, last) else nc.vector.tensor_copy
            copy_words(grouped[b].rearrange("p (e u) -> p e u", u=2), turned[b][:].rearrange("p u e -> p e u"))

        def multiply(b, held):
            val_codes = keep.tile([P, P], U32, align_bytes=64, tag=f"picked{b + 1}" if held else f"codes{b}")
            val_bytes = keep.tile([P, P], U8, align_bytes=64, name=f"val_bytes{b}")
            nc.vector.quantize_mx(out=val_codes[:].bitcast(FP8X4), scales=val_bytes[:], in_=grouped[b].bitcast(BF16))
            width = HALF if b == last else J
            pieces[b] = []
            for lo in range(0, J, width):
                sums = psum.tile([P, width], F32, tag="acc", bufs=6)
                nc.tensor.matmul_mx(
                    out=sums[:],
                    lhsT=val_codes[:].bitcast(FP8X4),
                    lhsT_scale=val_bytes[:],
                    rhs=table_codes[:, lo : lo + width].bitcast(FP8X4),
                    rhs_scale=table_bytes[:, lo : lo + width],
                    start=True,
                    stop=True,
                )
                pieces[b].append((lo, sums))

        def shift(b):
            for lo, sums in pieces[b]:
                n = min(sums.shape[1], J - 1 - lo)
                nc.vector.tensor_tensor(
                    shifted[b % 2][:, lo + 1 : lo + 1 + n], sums[:, :n], mem_wide[:, lo + 1 : lo + 1 + n], MULT
                )

        def finish(b):
            for lo, sums in pieces[b]:
                cols = slice(lo, lo + sums.shape[1])
                nc.vector.tensor_tensor(results[b][:, cols], sums[:], shifted[b % 2][:, cols], SUBTRACT)
                nc.sync.dma_start(out[b * P : (b + 1) * P, cols], results[b][:, cols])

        turn(0)
        group(0, False)
        multiply(0, False)
        turn(1)
        shift(0)
        finish(0)
        group(1, False)
        turn(2)
        multiply(1, True)
        group(2, False)
        multiply(2, False)
        turn(3)
        shift(1)
        shift(2)
        finish(1)
        group(3, True)
        multiply(3, False)
        finish(2)
        shift(3)
        finish(3)
